import numpy as np
import ml_dtypes


def mxq(x, axis, fmt="e4m3"):
    dtype, down = {"e4m3": (ml_dtypes.float8_e4m3fn, 7), "e5m2": (ml_dtypes.float8_e5m2, 14)}[fmt]
    v = np.moveaxis(np.asarray(x, np.float32).astype(ml_dtypes.bfloat16).astype(np.float64), axis, -1)
    blocks = v.reshape(v.shape[:-1] + (-1, 32))
    amax = np.abs(blocks).max(-1, keepdims=True)
    byte = np.maximum(np.where(amax > 0, np.frexp(amax)[1] - 1 + 127, 0) - down, 1)
    scale = np.exp2(byte - 127.0)
    codes = (blocks / scale).astype(np.float32).astype(dtype).astype(np.float64)
    return np.moveaxis((codes * scale).reshape(v.shape), -1, axis)


WIDE = False


def mx_kscale(k):
    if not WIDE:
        return np.ones(k)
    levels = np.array([10, -10, 5, -5, 0])
    if k % 512:
        return np.exp2(np.random.permutation(np.resize(levels, k // 32))).repeat(32)
    a = np.empty((k // 512, 16))
    for p in range(k // 512):
        a[p, :8] = np.random.permutation(np.resize(levels, 8))
        for g in range(8):
            far = levels[np.abs(levels - a[p, g]) >= 10]
            a[p, g + 8] = far[np.random.randint(len(far))]
    return np.exp2(a.ravel()).repeat(32)


def f64(x):
    return np.asarray(x).astype(np.float64)


def striped(idx):
    return np.tile(np.asarray(idx).reshape(-1, 16).T, (8, 1)).astype(np.uint16)


def unstriped(offs):
    return offs[:16].T.reshape(-1).astype(np.int64)


B, N, T, D, DV, NQ = 1, 512, 2048, 512, 512, 128


def setup_inputs():
    n = np.random.standard_normal
    idx = np.random.permutation(T)[:B * N]
    s = mx_kscale(D)[:, None]
    u = np.ones(T)
    u[idx] = mx_kscale(B * N)
    r = np.random.uniform(0.5, 2.0, T)
    long = np.random.uniform(0.9, 1.1, T)
    k = n((D, T)) / s * long
    v = n((DV, T)) / (u * r)
    return {
        "qT": (n((B, D, NQ)) * s * (0.90 / np.sqrt(D))).astype(np.float32),
        "kT": k.astype(np.float32),
        "vT": v.astype(np.float32),
        "vs": np.tile(u * r, (128, 1)).astype(np.float32),
        "kb": np.tile(-0.5 * np.sum(np.square(k * s), 0) * (0.90 / np.sqrt(D)), (128, 1)).astype(np.float32),
        "offs": striped(idx),
    }


def reference(qT, kT, vT, vs, kb, offs):
    idx = unstriped(offs)
    k = f64(kT)
    v = f64(vT)
    pick = lambda x: x[:, idx].reshape(x.shape[0], B, N).transpose(1, 0, 2)
    q = f64(qT)
    score = mxq(q, 1, "e4m3").transpose(0, 2, 1) @ mxq(pick(k), 1, "e4m3")
    score = score + pick(f64(kb))[:, :1, :]
    m = score.max(-1, keepdims=True)
    p = np.exp(score - m)
    total = p.sum(-1, keepdims=True)
    w = p * pick(f64(vs))[:, :1, :]
    y = mxq(w, 2, "e4m3") @ mxq(pick(v).transpose(0, 2, 1), 1, "e4m3")
    y = y / total
    return y

@@ -1,0 +1,185 @@
+from contextlib import ExitStack
+
+import concourse.mybir as mybir
+from concourse.masks import make_identity
+
+FLOPS = 2 * 2 * 128 * 512 * 512
+BYTES = 4 * (2 * 512 * 2048 + 2 * 2048 + 512 * 128 + 128 * 512) + 2 * 128 * 32
+
+F32 = mybir.dt.float32
+BF16 = mybir.dt.bfloat16
+U32 = mybir.dt.uint32
+U16 = mybir.dt.uint16
+U8 = mybir.dt.uint8
+FP8X4 = mybir.dt.float8_e4m3fn_x4
+
+P = 128
+POOL = 2048
+SLOTS = 512
+D = 512
+NQ = 128
+PACK = 4
+
+
+def tile_attend_rbf_topk_kernel(tc, qT, kT, vT, vs, kb, offs, out):
+    nc = tc.nc
+    exp = mybir.ActivationFunctionType.Exp
+    copy = mybir.ActivationFunctionType.Copy
+    mult, subtract, min_op = mybir.AluOpType.mult, mybir.AluOpType.subtract, mybir.AluOpType.min
+
+    with ExitStack() as ctx:
+        keep = ctx.enter_context(tc.tile_pool(name="keep", bufs=1))
+        psum = ctx.enter_context(tc.psum_pool(name="psum", bufs=2))
+
+        offsets = keep.tile([P, SLOTS // 16], U16, name="offsets")
+        nc.sync.dma_start(offsets[:], offs)
+
+        k_rows = kT.rearrange("(p t) w -> p t w", t=PACK)
+        k_win = [keep.tile([P, POOL], F32, name=f"k_win{t}") for t in range(PACK)]
+        v_win = [keep.tile([P, POOL], F32, name=f"v_win{b}") for b in range(4)]
+        q_raw = keep.tile([P, PACK, NQ], F32, name="q_raw")
+        kb_win = keep.tile([P, POOL], F32, name="kb_win")
+        vs_win = keep.tile([P, POOL], F32, name="vs_win")
+        nc.vector.memset(kb_win[:], 0.0)
+        nc.vector.memset(vs_win[:], 0.0)
+        nc.sync.dma_start(k_win[0][:], k_rows[:, 0, :])
+        nc.sync.dma_start(kb_win[0:1, :], kb[0:1, :])
+        nc.sync.dma_start(vs_win[0:1, :], vs[0:1, :])
+        nc.sync.dma_start(q_raw[:], qT[0].rearrange("(p t) w -> p t w", t=PACK))
+        for t in range(1, PACK):
+            nc.sync.dma_start(k_win[t][:], k_rows[:, t, :])
+        for b in range(4):
+            nc.sync.dma_start(v_win[b][:], vT[b * P : (b + 1) * P, :])
+
+        ident = keep.tile([P, P], F32, name="ident")
+        ident_bf = keep.tile([P, P], BF16, name="ident_bf")
+        make_identity(nc, ident[:])
+        nc.vector.tensor_copy(ident_bf[:], ident[:])
+
+        warm = keep.tile([P, 1], F32, name="warm")
+        nc.scalar.activation(warm[:], ident[:, 0:1], exp)
+
+        v_codes = keep.tile([P, 4, P], U32, name="v_codes", align_bytes=64)
+        v_scales = keep.tile([P, 4, P], U8, name="v_scales", align_bytes=64)
+        v_sb = [keep.tile([P, SLOTS], BF16, name=f"v_sb{b}") for b in range(4)]
+        v_grouped = [keep.tile([P, P, PACK], BF16, name=f"v_grouped{b}", align_bytes=64) for b in range(4)]
+
+        def gather_values(b):
+            nc.vector.tensor_copy(v_sb[b][:].rearrange("p (t b r) -> p b t r", t=PACK, r=8), v_win[b][:].indirect(offsets[:]))
+
+        def turn_values(b):
+            v_turn = psum.tile([P, PACK, P], BF16, name=f"v_turn{b}", tag="v_turn", bufs=2)
+            for t in range(PACK):
+                nc.tensor.transpose(v_turn[:, t, :], v_sb[b][:, t * P : (t + 1) * P], ident_bf[:])
+            nc.scalar.copy(v_grouped[b][:], v_turn[:].rearrange("p t e -> p e t"))
+
+        def quantize_values(b):
+            nc.vector.quantize_mx(out=v_codes[:, b, :].bitcast(FP8X4), scales=v_scales[:, b, :], in_=v_grouped[b][:].rearrange("p e t -> p (e t)"))
+
+        k_grouped = keep.tile([P, SLOTS, PACK], BF16, name="k_grouped", align_bytes=64)
+        nc.vector.tensor_copy(k_grouped[:, :, 0], k_win[0][:].indirect(offsets[:]))
+
+        kb_row = keep.tile([P, SLOTS], F32, name="kb_row")
+        nc.vector.tensor_copy(kb_row[:], kb_win[:].indirect(offsets[:]))
+        vs_row = keep.tile([P, SLOTS], F32, name="vs_row")
+        nc.vector.tensor_copy(vs_row[:], vs_win[:].indirect(offsets[:]))
+
+        q_grouped = keep.tile([P, NQ, PACK], BF16, name="q_grouped", align_bytes=64)
+        q_codes = keep.tile([P, NQ], U32, name="q_codes", align_bytes=64)
+        q_scales = keep.tile([P, NQ], U8, name="q_scales", align_bytes=64)
+        nc.scalar.copy(q_grouped[:], q_raw[:].rearrange("p t w -> p w t"))
+
+        kb_turn = psum.tile([P, 4, P], F32, name="kb_turn", tag="turn")
+        for b in range(4):
+            nc.tensor.transpose(kb_turn[:, b, :], kb_row[:, b * P : (b + 1) * P], ident[:])
+        kb_col = keep.tile([P, 4], F32, name="kb_col")
+        nc.scalar.copy(kb_col[:], kb_turn[:, :, 0])
+        kb_spread = psum.tile([P, 4, P], F32, name="kb_spread", tag="turn")
+        for b in range(4):
+            nc.tensor.transpose(kb_spread[:, b, :], kb_col[:, b : b + 1].to_broadcast([P, P]), ident[:])
+        kb_all = keep.tile([P, SLOTS], F32, name="kb_all")
+        nc.scalar.copy(kb_all[:], kb_spread[:].rearrange("p b s -> p (b s)"))
+
+        vs_perm = keep.tile([P, PACK, 16, 8], F32, name="vs_perm")
+        nc.scalar.copy(vs_perm[:], vs_row[:].rearrange("p (b t r) -> p t b r", t=PACK, r=8))
+        vs_turn = psum.tile([P, PACK, P], F32, name="vs_turn", tag="turn")
+        for t in range(PACK):
+            nc.tensor.transpose(vs_turn[:, t, :], vs_perm[:, t].rearrange("p b r -> p (b r)"), ident[:])
+        vs_col = keep.tile([P, PACK], F32, name="vs_col")
+        nc.scalar.copy(vs_col[:], vs_turn[:, :, 0])
+
+        nc.vector.quantize_mx(out=q_codes[:].bitcast(FP8X4), scales=q_scales[:], in_=q_grouped[:].rearrange("p w t -> p (w t)"))
+
+        nc.vector.tensor_copy(k_grouped[:, :, 1], k_win[1][:].indirect(offsets[:]))
+        nc.vector.tensor_copy(k_grouped[:, :, 2], k_win[2][:].indirect(offsets[:]))
+        nc.vector.tensor_copy(k_grouped[:, :, 3], k_win[3][:].indirect(offsets[:]))
+        k_codes = keep.tile([P, SLOTS], U32, name="k_codes", align_bytes=64)
+        k_scales = keep.tile([P, SLOTS], U8, name="k_scales", align_bytes=64)
+        nc.vector.quantize_mx(out=k_codes[:].bitcast(FP8X4), scales=k_scales[:], in_=k_grouped[:].rearrange("p w t -> p (w t)"))
+        score = psum.tile([NQ, SLOTS], F32, name="score", tag="score", bufs=1)
+        nc.tensor.matmul_mx(
+            out=score[:],
+            lhsT=q_codes[:].bitcast(FP8X4),
+            lhsT_scale=q_scales[:],
+            rhs=k_codes[:].bitcast(FP8X4),
+            rhs_scale=k_scales[:],
+            start=True,
+            stop=True,
+        )
+
+        v_bf = keep.tile([P, POOL], BF16, name="v_bf")
+        nc.scalar.activation(v_bf[:], v_win[0][:], copy)
+
+        neg = keep.tile([NQ, SLOTS], F32, name="neg")
+        nc.vector.scalar_tensor_tensor(neg[:], score[:], -1.0, kb_all[:], mult, subtract)
+        neg_m = keep.tile([NQ, 1], F32, name="neg_m")
+        nc.vector.tensor_reduce(neg_m[:], neg[:], axis=mybir.AxisListType.X, op=min_op)
+        p = keep.tile([NQ, PACK, 16, 8], F32, name="p")
+        total = keep.tile([NQ, 1], F32, name="total")
+        nc.scalar.activation(p[:], neg[:].rearrange("p (b t r) -> p t b r", t=PACK, r=8), exp, bias=neg_m[:], scale=-1.0, accum_out=total[:])
+        nc.scalar.activation(v_sb[0][:].rearrange("p (t b r) -> p b t r", t=PACK, r=8), v_bf[:].indirect(offsets[:]), copy)
+        gather_values(1)
+        p_turn = psum.tile([P, PACK, NQ], F32, name="p_turn", tag="turn")
+        for t in range(PACK):
+            nc.tensor.transpose(p_turn[:, t, :], p[:, t].rearrange("p b r -> p (b r)"), ident[:])
+        w_grouped = keep.tile([P, NQ, PACK], BF16, name="w_grouped", align_bytes=64)
+        nc.vector.tensor_tensor(
+            w_grouped[:],
+            p_turn[:].rearrange("p t q -> p q t"),
+            vs_col[:].unsqueeze(1).to_broadcast([P, NQ, PACK]),
+            mult,
+        )
+        turn_values(0)
+        turn_values(1)
+        gather_values(2)
+        w_codes = keep.tile([P, NQ], U32, name="w_codes", align_bytes=64)
+        w_scales = keep.tile([P, NQ], U8, name="w_scales", align_bytes=64)
+        nc.vector.quantize_mx(out=w_codes[:].bitcast(FP8X4), scales=w_scales[:], in_=w_grouped[:].rearrange("p w t -> p (w t)"))
+        quantize_values(0)
+        quantize_values(1)
+        turn_values(2)
+        inverse = keep.tile([NQ, 1], F32, name="inverse")
+        nc.vector.reciprocal(inverse[:], total[:])
+        gather_values(3)
+        quantize_values(2)
+        turn_values(3)
+        quantize_values(3)
+
+        def product(y, b):
+            nc.tensor.matmul_mx(
+                out=y,
+                lhsT=w_codes[:].bitcast(FP8X4),
+                lhsT_scale=w_scales[:],
+                rhs=v_codes[:, b, :].bitcast(FP8X4),
+                rhs_scale=v_scales[:, b, :],
+                start=True,
+                stop=True,
+            )
+
+        for half in range(2):
+            y = psum.tile([NQ, 2, P], F32, name=f"y{half}", tag="y")
+            product(y[:, 0, :], 2 * half)
+            product(y[:, 1, :], 2 * half + 1)
+            result = keep.tile([NQ, 2 * P], F32, name=f"result{half}")
+            nc.scalar.activation(result[:], y[:].rearrange("p b e -> p (b e)"), copy, scale=inverse[:])
+            nc.sync.dma_start(out[0, :, 2 * half * P : 2 * (half + 1) * P], result[:])

@@ -36,16 +36,16 @@ def tile_attend_rbf_topk_kernel(tc, qT, kT, vT, vs, kb, offs, out):
 
         k_rows = kT.rearrange("(p t) w -> p t w", t=PACK)
         k_win = [keep.tile([P, POOL], F32, name=f"k_win{t}") for t in range(PACK)]
-        v_win = [keep.tile([P, POOL], F32, name=f"v_win{b}") for b in range(4)]
+        v_win = [keep.tile([P, POOL], F32, name=f"v_win{b}", tag=f"v_win{b}", align_bytes=64) for b in range(4)]
         q_raw = keep.tile([P, PACK, NQ], F32, name="q_raw")
         kb_win = keep.tile([P, POOL], F32, name="kb_win")
         vs_win = keep.tile([P, POOL], F32, name="vs_win")
         nc.vector.memset(kb_win[:], 0.0)
-        nc.vector.memset(vs_win[:], 0.0)
+        nc.gpsimd.memset(vs_win[:], 0.0)
         nc.sync.dma_start(k_win[0][:], k_rows[:, 0, :])
+        nc.sync.dma_start(q_raw[:], qT[0].rearrange("(p t) w -> p t w", t=PACK))
         nc.sync.dma_start(kb_win[0:1, :], kb[0:1, :])
         nc.sync.dma_start(vs_win[0:1, :], vs[0:1, :])
-        nc.sync.dma_start(q_raw[:], qT[0].rearrange("(p t) w -> p t w", t=PACK))
         for t in range(1, PACK):
             nc.sync.dma_start(k_win[t][:], k_rows[:, t, :])
         for b in range(4):
@@ -59,25 +59,33 @@ def tile_attend_rbf_topk_kernel(tc, qT, kT, vT, vs, kb, offs, out):
         warm = keep.tile([P, 1], F32, name="warm")
         nc.scalar.activation(warm[:], ident[:, 0:1], exp)
 
-        v_codes = keep.tile([P, 4, P], U32, name="v_codes", align_bytes=64)
         v_scales = keep.tile([P, 4, P], U8, name="v_scales", align_bytes=64)
         v_sb = [keep.tile([P, SLOTS], BF16, name=f"v_sb{b}") for b in range(4)]
-        v_grouped = [keep.tile([P, P, PACK], BF16, name=f"v_grouped{b}", align_bytes=64) for b in range(4)]
+        v_grouped = keep.tile([P, 4, P, PACK], BF16, name="v_grouped", align_bytes=64)
 
         def gather_values(b):
             nc.vector.tensor_copy(v_sb[b][:].rearrange("p (t b r) -> p b t r", t=PACK, r=8), v_win[b][:].indirect(offsets[:]))
 
-        def turn_values(b):
+        def turn_values(b, copy_out):
             v_turn = psum.tile([P, PACK, P], BF16, name=f"v_turn{b}", tag="v_turn", bufs=2)
             for t in range(PACK):
                 nc.tensor.transpose(v_turn[:, t, :], v_sb[b][:, t * P : (t + 1) * P], ident_bf[:])
-            nc.scalar.copy(v_grouped[b][:], v_turn[:].rearrange("p t e -> p e t"))
+            copy_out(v_grouped[:, b], v_turn[:].rearrange("p t e -> p e t"))
 
-        def quantize_values(b):
-            nc.vector.quantize_mx(out=v_codes[:, b, :].bitcast(FP8X4), scales=v_scales[:, b, :], in_=v_grouped[b][:].rearrange("p e t -> p (e t)"))
+        v_codes = {}
+
+        def quantize_values(first, count, codes):
+            nc.vector.quantize_mx(
+                out=codes[:].rearrange("p b e -> p (b e)").bitcast(FP8X4),
+                scales=v_scales[:, first : first + count, :].rearrange("p b e -> p (b e)"),
+                in_=v_grouped[:, first : first + count].rearrange("p b e t -> p (b e t)"),
+            )
+            for b in range(count):
+                v_codes[first + b] = codes[:, b, :]
 
         k_grouped = keep.tile([P, SLOTS, PACK], BF16, name="k_grouped", align_bytes=64)
-        nc.vector.tensor_copy(k_grouped[:, :, 0], k_win[0][:].indirect(offsets[:]))
+        k_first = keep.tile([P, 2, SLOTS], F32, name="k_first")
+        nc.vector.tensor_copy(k_first[:, 0, :], k_win[0][:].indirect(offsets[:]))
 
         kb_row = keep.tile([P, SLOTS], F32, name="kb_row")
         nc.vector.tensor_copy(kb_row[:], kb_win[:].indirect(offsets[:]))
@@ -97,6 +105,11 @@ def tile_attend_rbf_topk_kernel(tc, qT, kT, vT, vs, kb, offs, out):
         kb_spread = psum.tile([P, 4, P], F32, name="kb_spread", tag="turn")
         for b in range(4):
             nc.tensor.transpose(kb_spread[:, b, :], kb_col[:, b : b + 1].to_broadcast([P, P]), ident[:])
+
+        nc.vector.quantize_mx(out=q_codes[:].bitcast(FP8X4), scales=q_scales[:], in_=q_grouped[:].rearrange("p w t -> p (w t)"))
+
+        nc.vector.tensor_copy(k_first[:, 1, :], k_win[1][:].indirect(offsets[:]))
+        nc.scalar.copy(k_grouped[:, :, 0:2], k_first[:].rearrange("p t w -> p w t"))
         kb_all = keep.tile([P, SLOTS], F32, name="kb_all")
         nc.scalar.copy(kb_all[:], kb_spread[:].rearrange("p b s -> p (b s)"))
 
@@ -108,9 +121,6 @@ def tile_attend_rbf_topk_kernel(tc, qT, kT, vT, vs, kb, offs, out):
         vs_col = keep.tile([P, PACK], F32, name="vs_col")
         nc.scalar.copy(vs_col[:], vs_turn[:, :, 0])
 
-        nc.vector.quantize_mx(out=q_codes[:].bitcast(FP8X4), scales=q_scales[:], in_=q_grouped[:].rearrange("p w t -> p (w t)"))
-
-        nc.vector.tensor_copy(k_grouped[:, :, 1], k_win[1][:].indirect(offsets[:]))
         nc.vector.tensor_copy(k_grouped[:, :, 2], k_win[2][:].indirect(offsets[:]))
         nc.vector.tensor_copy(k_grouped[:, :, 3], k_win[3][:].indirect(offsets[:]))
         k_codes = keep.tile([P, SLOTS], U32, name="k_codes", align_bytes=64)
@@ -127,50 +137,50 @@ def tile_attend_rbf_topk_kernel(tc, qT, kT, vT, vs, kb, offs, out):
             stop=True,
         )
 
-        v_bf = keep.tile([P, POOL], BF16, name="v_bf")
-        nc.scalar.activation(v_bf[:], v_win[0][:], copy)
+        gather_values(0)
+        turn_values(0, nc.scalar.copy)
 
-        neg = keep.tile([NQ, SLOTS], F32, name="neg")
+        neg = keep.tile([NQ, SLOTS], F32, name="neg", tag="v_win0", align_bytes=64)
         nc.vector.scalar_tensor_tensor(neg[:], score[:], -1.0, kb_all[:], mult, subtract)
         neg_m = keep.tile([NQ, 1], F32, name="neg_m")
         nc.vector.tensor_reduce(neg_m[:], neg[:], axis=mybir.AxisListType.X, op=min_op)
+        gather_values(1)
+        codes_0 = keep.tile([P, 1, P], U32, name="codes_0", align_bytes=64)
+        quantize_values(0, 1, codes_0)
         p = keep.tile([NQ, PACK, 16, 8], F32, name="p")
         total = keep.tile([NQ, 1], F32, name="total")
         nc.scalar.activation(p[:], neg[:].rearrange("p (b t r) -> p t b r", t=PACK, r=8), exp, bias=neg_m[:], scale=-1.0, accum_out=total[:])
-        nc.scalar.activation(v_sb[0][:].rearrange("p (t b r) -> p b t r", t=PACK, r=8), v_bf[:].indirect(offsets[:]), copy)
-        gather_values(1)
         p_turn = psum.tile([P, PACK, NQ], F32, name="p_turn", tag="turn")
         for t in range(PACK):
             nc.tensor.transpose(p_turn[:, t, :], p[:, t].rearrange("p b r -> p (b r)"), ident[:])
-        w_grouped = keep.tile([P, NQ, PACK], BF16, name="w_grouped", align_bytes=64)
+        turn_values(1, nc.scalar.copy)
+        gather_values(2)
+        w_grouped = keep.tile([P, NQ, PACK], BF16, name="w_grouped", tag="v_win2", align_bytes=64)
         nc.vector.tensor_tensor(
             w_grouped[:],
             p_turn[:].rearrange("p t q -> p q t"),
             vs_col[:].unsqueeze(1).to_broadcast([P, NQ, PACK]),
             mult,
         )
-        turn_values(0)
-        turn_values(1)
-        gather_values(2)
+        turn_values(2, nc.scalar.copy)
         w_codes = keep.tile([P, NQ], U32, name="w_codes", align_bytes=64)
         w_scales = keep.tile([P, NQ], U8, name="w_scales", align_bytes=64)
         nc.vector.quantize_mx(out=w_codes[:].bitcast(FP8X4), scales=w_scales[:], in_=w_grouped[:].rearrange("p w t -> p (w t)"))
-        quantize_values(0)
-        quantize_values(1)
-        turn_values(2)
         inverse = keep.tile([NQ, 1], F32, name="inverse")
-        nc.vector.reciprocal(inverse[:], total[:])
         gather_values(3)
-        quantize_values(2)
-        turn_values(3)
-        quantize_values(3)
+        nc.vector.reciprocal(inverse[:], total[:])
+        codes_12 = keep.tile([P, 2, P], U32, name="codes_12", tag="v_win3", align_bytes=64)
+        quantize_values(1, 2, codes_12)
+        turn_values(3, nc.vector.tensor_copy)
+        codes_3 = keep.tile([P, 1, P], U32, name="codes_3", align_bytes=64)
+        quantize_values(3, 1, codes_3)
 
         def product(y, b):
             nc.tensor.matmul_mx(
                 out=y,
                 lhsT=w_codes[:].bitcast(FP8X4),
                 lhsT_scale=w_scales[:],
-                rhs=v_codes[:, b, :].bitcast(FP8X4),
+                rhs=v_codes[b].bitcast(FP8X4),
                 rhs_scale=v_scales[:, b, :],
                 start=True,
                 stop=True,

@@ -44,9 +44,11 @@ def tile_attend_rbf_topk_kernel(tc, qT, kT, vT, vs, kb, offs, out):
         nc.gpsimd.memset(vs_win[:], 0.0)
         nc.sync.dma_start(k_win[0][:], k_rows[:, 0, :])
         nc.sync.dma_start(q_raw[:], qT[0].rearrange("(p t) w -> p t w", t=PACK))
+        nc.sync.dma_start(k_win[1][:, 0 : POOL // 2], k_rows[:, 1, 0 : POOL // 2])
         nc.sync.dma_start(kb_win[0:1, :], kb[0:1, :])
         nc.sync.dma_start(vs_win[0:1, :], vs[0:1, :])
-        for t in range(1, PACK):
+        nc.sync.dma_start(k_win[1][:, POOL // 2 :], k_rows[:, 1, POOL // 2 :])
+        for t in range(2, PACK):
             nc.sync.dma_start(k_win[t][:], k_rows[:, t, :])
         for b in range(4):
             nc.sync.dma_start(v_win[b][:], vT[b * P : (b + 1) * P, :])
@@ -171,7 +173,7 @@ def tile_attend_rbf_topk_kernel(tc, qT, kT, vT, vs, kb, offs, out):
         nc.vector.reciprocal(inverse[:], total[:])
         codes_12 = keep.tile([P, 2, P], U32, name="codes_12", tag="v_win3", align_bytes=64)
         quantize_values(1, 2, codes_12)
-        turn_values(3, nc.vector.tensor_copy)
+        turn_values(3, nc.scalar.copy)
         codes_3 = keep.tile([P, 1, P], U32, name="codes_3", align_bytes=64)
         quantize_values(3, 1, codes_3)
 
@@ -186,10 +188,10 @@ def tile_attend_rbf_topk_kernel(tc, qT, kT, vT, vs, kb, offs, out):
                 stop=True,
             )
 
-        for half in range(2):
-            y = psum.tile([NQ, 2, P], F32, name=f"y{half}", tag="y")
-            product(y[:, 0, :], 2 * half)
-            product(y[:, 1, :], 2 * half + 1)
-            result = keep.tile([NQ, 2 * P], F32, name=f"result{half}")
+        for first, count in ((0, 3), (3, 1)):
+            y = psum.tile([NQ, count, P], F32, name=f"y{first}", tag="y")
+            for b in range(count):
+                product(y[:, b, :], first + b)
+            result = keep.tile([NQ, count * P], F32, name=f"result{first}")
             nc.scalar.activation(result[:], y[:].rearrange("p b e -> p (b e)"), copy, scale=inverse[:])
-            nc.sync.dma_start(out[0, :, 2 * half * P : 2 * (half + 1) * P], result[:])
+            nc.sync.dma_start(out[0, :, first * P : (first + count) * P], result[:])

@@ -29,6 +29,7 @@ def tile_attend_rbf_topk_kernel(tc, qT, kT, vT, vs, kb, offs, out):
 
     with ExitStack() as ctx:
         keep = ctx.enter_context(tc.tile_pool(name="keep", bufs=1))
+        over = ctx.enter_context(tc.tile_pool(name="over", bufs=1))
         psum = ctx.enter_context(tc.psum_pool(name="psum", bufs=2))
 
         offsets = keep.tile([P, SLOTS // 16], U16, name="offsets")
@@ -36,7 +37,8 @@ def tile_attend_rbf_topk_kernel(tc, qT, kT, vT, vs, kb, offs, out):
 
         k_rows = kT.rearrange("(p t) w -> p t w", t=PACK)
         k_win = [keep.tile([P, POOL], F32, name=f"k_win{t}") for t in range(PACK)]
-        v_win = [keep.tile([P, POOL], F32, name=f"v_win{b}", tag=f"v_win{b}", align_bytes=64) for b in range(4)]
+        v_win = [keep.tile([P, POOL], F32, name=f"v_win{b}", tag=f"v_win{b}", align_bytes=64) for b in range(3)]
+        v_win.append(over.tile([P, POOL], F32, name="v_win3", offset=0, align_bytes=64))
         q_raw = keep.tile([P, PACK, NQ], F32, name="q_raw")
         kb_win = keep.tile([P, POOL], F32, name="kb_win")
         vs_win = keep.tile([P, POOL], F32, name="vs_win")
@@ -78,12 +80,12 @@ def tile_attend_rbf_topk_kernel(tc, qT, kT, vT, vs, kb, offs, out):
 
         def quantize_values(first, count, codes):
             nc.vector.quantize_mx(
-                out=codes[:].rearrange("p b e -> p (b e)").bitcast(FP8X4),
+                out=codes.bitcast(FP8X4),
                 scales=v_scales[:, first : first + count, :].rearrange("p b e -> p (b e)"),
                 in_=v_grouped[:, first : first + count].rearrange("p b e t -> p (b e t)"),
             )
             for b in range(count):
-                v_codes[first + b] = codes[:, b, :]
+                v_codes[first + b] = codes[:, b * P : (b + 1) * P]
 
         k_grouped = keep.tile([P, SLOTS, PACK], BF16, name="k_grouped", align_bytes=64)
         k_first = keep.tile([P, 2, SLOTS], F32, name="k_first")
@@ -147,8 +149,8 @@ def tile_attend_rbf_topk_kernel(tc, qT, kT, vT, vs, kb, offs, out):
         neg_m = keep.tile([NQ, 1], F32, name="neg_m")
         nc.vector.tensor_reduce(neg_m[:], neg[:], axis=mybir.AxisListType.X, op=min_op)
         gather_values(1)
-        codes_0 = keep.tile([P, 1, P], U32, name="codes_0", align_bytes=64)
-        quantize_values(0, 1, codes_0)
+        codes_0 = keep.tile([P, P], U32, name="codes_0", align_bytes=64)
+        quantize_values(0, 1, codes_0[:])
         p = keep.tile([NQ, PACK, 16, 8], F32, name="p")
         total = keep.tile([NQ, 1], F32, name="total")
         nc.scalar.activation(p[:], neg[:].rearrange("p (b t r) -> p t b r", t=PACK, r=8), exp, bias=neg_m[:], scale=-1.0, accum_out=total[:])
@@ -157,7 +159,8 @@ def tile_attend_rbf_topk_kernel(tc, qT, kT, vT, vs, kb, offs, out):
             nc.tensor.transpose(p_turn[:, t, :], p[:, t].rearrange("p b r -> p (b r)"), ident[:])
         turn_values(1, nc.scalar.copy)
         gather_values(2)
-        w_grouped = keep.tile([P, NQ, PACK], BF16, name="w_grouped", tag="v_win2", align_bytes=64)
+        gather_values(3)
+        w_grouped = over.tile([P, NQ, PACK], BF16, name="w_grouped", offset=0, align_bytes=64)
         nc.vector.tensor_tensor(
             w_grouped[:],
             p_turn[:].rearrange("p t q -> p q t"),
@@ -167,15 +170,14 @@ def tile_attend_rbf_topk_kernel(tc, qT, kT, vT, vs, kb, offs, out):
         turn_values(2, nc.scalar.copy)
         w_codes = keep.tile([P, NQ], U32, name="w_codes", align_bytes=64)
         w_scales = keep.tile([P, NQ], U8, name="w_scales", align_bytes=64)
-        nc.vector.quantize_mx(out=w_codes[:].bitcast(FP8X4), scales=w_scales[:], in_=w_grouped[:].rearrange("p w t -> p (w t)"))
+        nc.vector.quantize_mx(out=w_codes[:].bitcast(FP8X4), scales=w_scales[:], in_=w_grouped[:].rearrange("p q t -> p (q t)"))
         inverse = keep.tile([NQ, 1], F32, name="inverse")
-        gather_values(3)
         nc.vector.reciprocal(inverse[:], total[:])
-        codes_12 = keep.tile([P, 2, P], U32, name="codes_12", tag="v_win3", align_bytes=64)
-        quantize_values(1, 2, codes_12)
+        codes_12 = over.tile([P, 2 * P], U32, name="codes_12", offset=2 * NQ * PACK, align_bytes=64)
+        quantize_values(1, 2, codes_12[:])
         turn_values(3, nc.scalar.copy)
-        codes_3 = keep.tile([P, 1, P], U32, name="codes_3", align_bytes=64)
-        quantize_values(3, 1, codes_3)
+        codes_3 = keep.tile([P, P], U32, name="codes_3", align_bytes=64)
+        quantize_values(3, 1, codes_3[:])
 
         def product(y, b):
             nc.tensor.matmul_mx(
@@ -193,5 +195,8 @@ def tile_attend_rbf_topk_kernel(tc, qT, kT, vT, vs, kb, offs, out):
             for b in range(count):
                 product(y[:, b, :], first + b)
             result = keep.tile([NQ, count * P], F32, name=f"result{first}")
-            nc.scalar.activation(result[:], y[:].rearrange("p b e -> p (b e)"), copy, scale=inverse[:])
+            if first == 0:
+                nc.scalar.activation(result[:], y[:].rearrange("p b e -> p (b e)"), copy, scale=inverse[:])
+            else:
+                nc.vector.tensor_scalar(result[:], y[:].rearrange("p b e -> p (b e)"), inverse[:], None, mult)
             nc.sync.dma_start(out[0, :, first * P : (first + count) * P], result[:])

@@ -3,9 +3,6 @@ from contextlib import ExitStack
 import concourse.mybir as mybir
 from concourse.masks import make_identity
 
-FLOPS = 2 * 2 * 128 * 512 * 512
-BYTES = 4 * (2 * 512 * 2048 + 2 * 2048 + 512 * 128 + 128 * 512) + 2 * 128 * 32
-
 F32 = mybir.dt.float32
 BF16 = mybir.dt.bfloat16
 U32 = mybir.dt.uint32
@@ -16,16 +13,23 @@ FP8X4 = mybir.dt.float8_e4m3fn_x4
 P = 128
 POOL = 2048
 SLOTS = 512
-D = 512
 NQ = 128
+D = 512
+DV = 512
 PACK = 4
+PAIRS = 2
+BLOCKS = DV // P
+COLS = SLOTS // P
+
+FLOPS = 2 * NQ * SLOTS * (D + DV)
+BYTES = 4 * ((D + DV) * POOL + 2 * POOL + D * NQ + NQ * DV) + 2 * P * (SLOTS // 16)
 
 
 def tile_attend_rbf_topk_kernel(tc, qT, kT, vT, vs, kb, offs, out):
     nc = tc.nc
     exp = mybir.ActivationFunctionType.Exp
     copy = mybir.ActivationFunctionType.Copy
-    mult, subtract, min_op = mybir.AluOpType.mult, mybir.AluOpType.subtract, mybir.AluOpType.min
+    mult, subtract, minimum = mybir.AluOpType.mult, mybir.AluOpType.subtract, mybir.AluOpType.min
 
     with ExitStack() as ctx:
         keep = ctx.enter_context(tc.tile_pool(name="keep", bufs=1))
@@ -35,48 +39,49 @@ def tile_attend_rbf_topk_kernel(tc, qT, kT, vT, vs, kb, offs, out):
         offsets = keep.tile([P, SLOTS // 16], U16, name="offsets")
         nc.sync.dma_start(offsets[:], offs)
 
-        k_rows = kT.rearrange("(p t) w -> p t w", t=PACK)
+        k_rows = kT.rearrange("(m t) w -> m t w", t=PACK)
         k_win = [keep.tile([P, POOL], F32, name=f"k_win{t}") for t in range(PACK)]
-        v_win = [keep.tile([P, POOL], F32, name=f"v_win{b}", tag=f"v_win{b}", align_bytes=64) for b in range(3)]
-        v_win.append(over.tile([P, POOL], F32, name="v_win3", offset=0, align_bytes=64))
+        v_win = [keep.tile([P, POOL], F32, name=f"v_win{b}", tag=f"v_win{b}", align_bytes=64) for b in range(BLOCKS - 1)]
+        v_win.append(over.tile([P, POOL], F32, name=f"v_win{BLOCKS - 1}", offset=0, align_bytes=64))
         q_raw = keep.tile([P, PACK, NQ], F32, name="q_raw")
         kb_win = keep.tile([P, POOL], F32, name="kb_win")
         vs_win = keep.tile([P, POOL], F32, name="vs_win")
         nc.vector.memset(kb_win[:], 0.0)
         nc.gpsimd.memset(vs_win[:], 0.0)
         nc.sync.dma_start(k_win[0][:], k_rows[:, 0, :])
-        nc.sync.dma_start(q_raw[:], qT[0].rearrange("(p t) w -> p t w", t=PACK))
+        nc.sync.dma_start(q_raw[:], qT[0].rearrange("(m t) q -> m t q", t=PACK))
         nc.sync.dma_start(k_win[1][:, 0 : POOL // 2], k_rows[:, 1, 0 : POOL // 2])
         nc.sync.dma_start(kb_win[0:1, :], kb[0:1, :])
         nc.sync.dma_start(vs_win[0:1, :], vs[0:1, :])
         nc.sync.dma_start(k_win[1][:, POOL // 2 :], k_rows[:, 1, POOL // 2 :])
         for t in range(2, PACK):
             nc.sync.dma_start(k_win[t][:], k_rows[:, t, :])
-        for b in range(4):
+        for b in range(BLOCKS):
             nc.sync.dma_start(v_win[b][:], vT[b * P : (b + 1) * P, :])
 
         ident = keep.tile([P, P], F32, name="ident")
-        ident_bf = keep.tile([P, P], BF16, name="ident_bf")
         make_identity(nc, ident[:])
-        nc.vector.tensor_copy(ident_bf[:], ident[:])
 
         warm = keep.tile([P, 1], F32, name="warm")
         nc.scalar.activation(warm[:], ident[:, 0:1], exp)
 
-        v_scales = keep.tile([P, 4, P], U8, name="v_scales", align_bytes=64)
-        v_sb = [keep.tile([P, SLOTS], BF16, name=f"v_sb{b}") for b in range(4)]
-        v_grouped = keep.tile([P, 4, P, PACK], BF16, name="v_grouped", align_bytes=64)
+        v_scales = keep.tile([P, BLOCKS, P], U8, name="v_scales", align_bytes=64)
+        v_sb = [keep.tile([P, SLOTS], BF16, name=f"v_sb{b}") for b in range(BLOCKS)]
+        v_grouped = keep.tile([P, BLOCKS, P, PACK], BF16, name="v_grouped", align_bytes=64)
+        v_codes = {}
 
         def gather_values(b):
-            nc.vector.tensor_copy(v_sb[b][:].rearrange("p (t b r) -> p b t r", t=PACK, r=8), v_win[b][:].indirect(offsets[:]))
+            nc.vector.tensor_copy(v_sb[b][:].rearrange("p (u m h) -> p m u h", u=PAIRS, h=2), v_win[b][:].indirect(offsets[:]))
 
-        def turn_values(b, copy_out):
-            v_turn = psum.tile([P, PACK, P], BF16, name=f"v_turn{b}", tag="v_turn", bufs=2)
-            for t in range(PACK):
-                nc.tensor.transpose(v_turn[:, t, :], v_sb[b][:, t * P : (t + 1) * P], ident_bf[:])
-            copy_out(v_grouped[:, b], v_turn[:].rearrange("p t e -> p e t"))
-
-        v_codes = {}
+        def turn_values(b):
+            words = v_sb[b][:].bitcast(F32)
+            v_turn = psum.tile([P, PAIRS, P], F32, name=f"v_turn{b}", tag="v_turn", bufs=2)
+            for u in range(PAIRS):
+                nc.tensor.transpose(v_turn[:, u, :], words[:, u * P : (u + 1) * P], ident[:])
+            nc.scalar.copy(
+                v_grouped[:, b].rearrange("p e t -> p (e t)").bitcast(F32).rearrange("p (e u) -> p e u", u=PAIRS),
+                v_turn[:].rearrange("p u e -> p e u"),
+            )
 
         def quantize_values(first, count, codes):
             nc.vector.quantize_mx(
@@ -99,37 +104,37 @@ def tile_attend_rbf_topk_kernel(tc, qT, kT, vT, vs, kb, offs, out):
         q_grouped = keep.tile([P, NQ, PACK], BF16, name="q_grouped", align_bytes=64)
         q_codes = keep.tile([P, NQ], U32, name="q_codes", align_bytes=64)
         q_scales = keep.tile([P, NQ], U8, name="q_scales", align_bytes=64)
-        nc.scalar.copy(q_grouped[:], q_raw[:].rearrange("p t w -> p w t"))
+        nc.scalar.copy(q_grouped[:], q_raw[:].rearrange("p t q -> p q t"))
 
-        kb_turn = psum.tile([P, 4, P], F32, name="kb_turn", tag="turn")
-        for b in range(4):
-            nc.tensor.transpose(kb_turn[:, b, :], kb_row[:, b * P : (b + 1) * P], ident[:])
-        kb_col = keep.tile([P, 4], F32, name="kb_col")
+        kb_turn = psum.tile([P, COLS, P], F32, name="kb_turn", tag="turn")
+        for c in range(COLS):
+            nc.tensor.transpose(kb_turn[:, c, :], kb_row[:, c * P : (c + 1) * P], ident[:])
+        kb_col = keep.tile([P, COLS], F32, name="kb_col")
         nc.scalar.copy(kb_col[:], kb_turn[:, :, 0])
-        kb_spread = psum.tile([P, 4, P], F32, name="kb_spread", tag="turn")
-        for b in range(4):
-            nc.tensor.transpose(kb_spread[:, b, :], kb_col[:, b : b + 1].to_broadcast([P, P]), ident[:])
+        kb_spread = psum.tile([P, COLS, P], F32, name="kb_spread", tag="turn")
+        for c in range(COLS):
+            nc.tensor.transpose(kb_spread[:, c, :], kb_col[:, c : c + 1].to_broadcast([P, P]), ident[:])
 
-        nc.vector.quantize_mx(out=q_codes[:].bitcast(FP8X4), scales=q_scales[:], in_=q_grouped[:].rearrange("p w t -> p (w t)"))
+        nc.vector.quantize_mx(out=q_codes[:].bitcast(FP8X4), scales=q_scales[:], in_=q_grouped[:].rearrange("p q t -> p (q t)"))
 
         nc.vector.tensor_copy(k_first[:, 1, :], k_win[1][:].indirect(offsets[:]))
-        nc.scalar.copy(k_grouped[:, :, 0:2], k_first[:].rearrange("p t w -> p w t"))
+        nc.scalar.copy(k_grouped[:, :, 0:2], k_first[:].rearrange("p t i -> p i t"))
         kb_all = keep.tile([P, SLOTS], F32, name="kb_all")
-        nc.scalar.copy(kb_all[:], kb_spread[:].rearrange("p b s -> p (b s)"))
+        nc.scalar.copy(kb_all[:], kb_spread[:].rearrange("p c i -> p (c i)"))
 
-        vs_perm = keep.tile([P, PACK, 16, 8], F32, name="vs_perm")
-        nc.scalar.copy(vs_perm[:], vs_row[:].rearrange("p (b t r) -> p t b r", t=PACK, r=8))
+        vs_perm = keep.tile([P, PACK, P], F32, name="vs_perm")
+        nc.scalar.copy(vs_perm[:].rearrange("p t m -> p m t"), vs_row[:].rearrange("p (m t) -> p m t", t=PACK))
         vs_turn = psum.tile([P, PACK, P], F32, name="vs_turn", tag="turn")
         for t in range(PACK):
-            nc.tensor.transpose(vs_turn[:, t, :], vs_perm[:, t].rearrange("p b r -> p (b r)"), ident[:])
+            nc.tensor.transpose(vs_turn[:, t, :], vs_perm[:, t, :], ident[:])
         vs_col = keep.tile([P, PACK], F32, name="vs_col")
         nc.scalar.copy(vs_col[:], vs_turn[:, :, 0])
 
-        nc.vector.tensor_copy(k_grouped[:, :, 2], k_win[2][:].indirect(offsets[:]))
-        nc.vector.tensor_copy(k_grouped[:, :, 3], k_win[3][:].indirect(offsets[:]))
+        for t in range(2, PACK):
+            nc.vector.tensor_copy(k_grouped[:, :, t], k_win[t][:].indirect(offsets[:]))
         k_codes = keep.tile([P, SLOTS], U32, name="k_codes", align_bytes=64)
         k_scales = keep.tile([P, SLOTS], U8, name="k_scales", align_bytes=64)
-        nc.vector.quantize_mx(out=k_codes[:].bitcast(FP8X4), scales=k_scales[:], in_=k_grouped[:].rearrange("p w t -> p (w t)"))
+        nc.vector.quantize_mx(out=k_codes[:].bitcast(FP8X4), scales=k_scales[:], in_=k_grouped[:].rearrange("p i t -> p (i t)"))
         score = psum.tile([NQ, SLOTS], F32, name="score", tag="score", bufs=1)
         nc.tensor.matmul_mx(
             out=score[:],
@@ -142,40 +147,49 @@ def tile_attend_rbf_topk_kernel(tc, qT, kT, vT, vs, kb, offs, out):
         )
 
         gather_values(0)
-        turn_values(0, nc.scalar.copy)
+        turn_values(0)
 
         neg = keep.tile([NQ, SLOTS], F32, name="neg", tag="v_win0", align_bytes=64)
         nc.vector.scalar_tensor_tensor(neg[:], score[:], -1.0, kb_all[:], mult, subtract)
         neg_m = keep.tile([NQ, 1], F32, name="neg_m")
-        nc.vector.tensor_reduce(neg_m[:], neg[:], axis=mybir.AxisListType.X, op=min_op)
+        nc.vector.tensor_reduce(neg_m[:], neg[:], axis=mybir.AxisListType.X, op=minimum)
         gather_values(1)
         codes_0 = keep.tile([P, P], U32, name="codes_0", align_bytes=64)
         quantize_values(0, 1, codes_0[:])
-        p = keep.tile([NQ, PACK, 16, 8], F32, name="p")
+
+        p = keep.tile([NQ, PACK, P], F32, name="p")
         total = keep.tile([NQ, 1], F32, name="total")
-        nc.scalar.activation(p[:], neg[:].rearrange("p (b t r) -> p t b r", t=PACK, r=8), exp, bias=neg_m[:], scale=-1.0, accum_out=total[:])
+        nc.scalar.activation(
+            p[:].rearrange("q t m -> q m t"),
+            neg[:].rearrange("q (m t) -> q m t", t=PACK),
+            exp,
+            bias=neg_m[:],
+            scale=-1.0,
+            accum_out=total[:],
+        )
         p_turn = psum.tile([P, PACK, NQ], F32, name="p_turn", tag="turn")
         for t in range(PACK):
-            nc.tensor.transpose(p_turn[:, t, :], p[:, t].rearrange("p b r -> p (b r)"), ident[:])
-        turn_values(1, nc.scalar.copy)
+            nc.tensor.transpose(p_turn[:, t, :], p[:, t, :], ident[:])
+        turn_values(1)
         gather_values(2)
         gather_values(3)
+
         w_grouped = over.tile([P, NQ, PACK], BF16, name="w_grouped", offset=0, align_bytes=64)
         nc.vector.tensor_tensor(
             w_grouped[:],
-            p_turn[:].rearrange("p t q -> p q t"),
+            p_turn[:].rearrange("m t q -> m q t"),
             vs_col[:].unsqueeze(1).to_broadcast([P, NQ, PACK]),
             mult,
         )
-        turn_values(2, nc.scalar.copy)
+        turn_values(2)
+        codes_12 = over.tile([P, 2 * P], U32, name="codes_12", offset=2 * NQ * PACK, align_bytes=64)
+        quantize_values(1, 2, codes_12[:])
         w_codes = keep.tile([P, NQ], U32, name="w_codes", align_bytes=64)
         w_scales = keep.tile([P, NQ], U8, name="w_scales", align_bytes=64)
         nc.vector.quantize_mx(out=w_codes[:].bitcast(FP8X4), scales=w_scales[:], in_=w_grouped[:].rearrange("p q t -> p (q t)"))
         inverse = keep.tile([NQ, 1], F32, name="inverse")
         nc.vector.reciprocal(inverse[:], total[:])
-        codes_12 = over.tile([P, 2 * P], U32, name="codes_12", offset=2 * NQ * PACK, align_bytes=64)
-        quantize_values(1, 2, codes_12[:])
-        turn_values(3, nc.scalar.copy)
+        turn_values(3)
         codes_3 = keep.tile([P, P], U32, name="codes_3", align_bytes=64)
         quantize_values(3, 1, codes_3[:])
 
@@ -190,13 +204,16 @@ def tile_attend_rbf_topk_kernel(tc, qT, kT, vT, vs, kb, offs, out):
                 stop=True,
             )
 
-        for first, count in ((0, 3), (3, 1)):
-            y = psum.tile([NQ, count, P], F32, name=f"y{first}", tag="y")
-            for b in range(count):
-                product(y[:, b, :], first + b)
-            result = keep.tile([NQ, count * P], F32, name=f"result{first}")
-            if first == 0:
-                nc.scalar.activation(result[:], y[:].rearrange("p b e -> p (b e)"), copy, scale=inverse[:])
-            else:
-                nc.vector.tensor_scalar(result[:], y[:].rearrange("p b e -> p (b e)"), inverse[:], None, mult)
-            nc.sync.dma_start(out[0, :, first * P : (first + count) * P], result[:])
+        y_first = psum.tile([NQ, 2, P], F32, name="y_first", tag="y")
+        y_last = psum.tile([NQ, 2, P], F32, name="y_last", tag="y")
+        for b in range(2):
+            product(y_first[:, b, :], b)
+        out_first = keep.tile([NQ, 2 * P], F32, name="out_first")
+        nc.scalar.activation(out_first[:], y_first[:].rearrange("q b e -> q (b e)"), copy, scale=inverse[:])
+        nc.scalar.dma_start(out[0, :, 0 : 2 * P], out_first[:])
+
+        for b in range(2):
+            product(y_last[:, b, :], 2 + b)
+        out_last = keep.tile([NQ, 2 * P], F32, name="out_last")
+        nc.vector.tensor_scalar(out_last[:], y_last[:].rearrange("q b e -> q (b e)"), inverse[:], None, mult)
+        nc.sync.dma_start(out[0, :, 2 * P : DV], out_last[:])

from contextlib import ExitStack

import concourse.mybir as mybir
from concourse.masks import make_identity

F32 = mybir.dt.float32
BF16 = mybir.dt.bfloat16
U32 = mybir.dt.uint32
U16 = mybir.dt.uint16
U8 = mybir.dt.uint8
FP8X4 = mybir.dt.float8_e4m3fn_x4

P = 128
POOL = 2048
SLOTS = 512
NQ = 128
D = 512
DV = 512
PACK = 4
PAIRS = 2
BLOCKS = DV // P
COLS = SLOTS // P

FLOPS = 2 * NQ * SLOTS * (D + DV)
BYTES = 4 * ((D + DV) * POOL + 2 * POOL + D * NQ + NQ * DV) + 2 * P * (SLOTS // 16)


def tile_attend_rbf_topk_kernel(tc, qT, kT, vT, vs, kb, offs, out):
    nc = tc.nc
    exp = mybir.ActivationFunctionType.Exp
    copy = mybir.ActivationFunctionType.Copy
    mult, subtract, minimum = mybir.AluOpType.mult, mybir.AluOpType.subtract, mybir.AluOpType.min

    with ExitStack() as ctx:
        keep = ctx.enter_context(tc.tile_pool(name="keep", bufs=1))
        over = ctx.enter_context(tc.tile_pool(name="over", bufs=1))
        psum = ctx.enter_context(tc.psum_pool(name="psum", bufs=2))

        offsets = keep.tile([P, SLOTS // 16], U16, name="offsets")
        nc.sync.dma_start(offsets[:], offs)

        k_rows = kT.rearrange("(m t) w -> m t w", t=PACK)
        k_win = [keep.tile([P, POOL], F32, name=f"k_win{t}") for t in range(PACK)]
        v_win = [keep.tile([P, POOL], F32, name=f"v_win{b}", tag=f"v_win{b}", align_bytes=64) for b in range(BLOCKS - 1)]
        v_win.append(over.tile([P, POOL], F32, name=f"v_win{BLOCKS - 1}", offset=0, align_bytes=64))
        q_raw = keep.tile([P, PACK, NQ], F32, name="q_raw")
        kb_win = keep.tile([P, POOL], F32, name="kb_win")
        vs_win = keep.tile([P, POOL], F32, name="vs_win")
        nc.vector.memset(kb_win[:], 0.0)
        nc.gpsimd.memset(vs_win[:], 0.0)
        nc.sync.dma_start(k_win[0][:], k_rows[:, 0, :])
        nc.sync.dma_start(q_raw[:], qT[0].rearrange("(m t) q -> m t q", t=PACK))
        nc.sync.dma_start(k_win[1][:, 0 : POOL // 2], k_rows[:, 1, 0 : POOL // 2])
        nc.sync.dma_start(kb_win[0:1, :], kb[0:1, :])
        nc.sync.dma_start(vs_win[0:1, :], vs[0:1, :])
        nc.sync.dma_start(k_win[1][:, POOL // 2 :], k_rows[:, 1, POOL // 2 :])
        for t in range(2, PACK):
            nc.sync.dma_start(k_win[t][:], k_rows[:, t, :])
        for b in range(BLOCKS):
            nc.sync.dma_start(v_win[b][:], vT[b * P : (b + 1) * P, :])

        ident = keep.tile([P, P], F32, name="ident")
        make_identity(nc, ident[:])

        warm = keep.tile([P, 1], F32, name="warm")
        nc.scalar.activation(warm[:], ident[:, 0:1], exp)

        v_scales = keep.tile([P, BLOCKS, P], U8, name="v_scales", align_bytes=64)
        v_sb = [keep.tile([P, SLOTS], BF16, name=f"v_sb{b}") for b in range(BLOCKS)]
        v_grouped = keep.tile([P, BLOCKS, P, PACK], BF16, name="v_grouped", align_bytes=64)
        v_codes = {}

        def gather_values(b):
            nc.vector.tensor_copy(v_sb[b][:].rearrange("p (u m h) -> p m u h", u=PAIRS, h=2), v_win[b][:].indirect(offsets[:]))

        def turn_values(b):
            words = v_sb[b][:].bitcast(F32)
            v_turn = psum.tile([P, PAIRS, P], F32, name=f"v_turn{b}", tag="v_turn", bufs=2)
            for u in range(PAIRS):
                nc.tensor.transpose(v_turn[:, u, :], words[:, u * P : (u + 1) * P], ident[:])
            nc.scalar.copy(
                v_grouped[:, b].rearrange("p e t -> p (e t)").bitcast(F32).rearrange("p (e u) -> p e u", u=PAIRS),
                v_turn[:].rearrange("p u e -> p e u"),
            )

        def quantize_values(first, count, codes):
            nc.vector.quantize_mx(
                out=codes.bitcast(FP8X4),
                scales=v_scales[:, first : first + count, :].rearrange("p b e -> p (b e)"),
                in_=v_grouped[:, first : first + count].rearrange("p b e t -> p (b e t)"),
            )
            for b in range(count):
                v_codes[first + b] = codes[:, b * P : (b + 1) * P]

        k_grouped = keep.tile([P, SLOTS, PACK], BF16, name="k_grouped", align_bytes=64)
        k_first = keep.tile([P, 2, SLOTS], F32, name="k_first")
        nc.vector.tensor_copy(k_first[:, 0, :], k_win[0][:].indirect(offsets[:]))

        kb_row = keep.tile([P, SLOTS], F32, name="kb_row")
        nc.vector.tensor_copy(kb_row[:], kb_win[:].indirect(offsets[:]))
        vs_row = keep.tile([P, SLOTS], F32, name="vs_row")
        nc.vector.tensor_copy(vs_row[:], vs_win[:].indirect(offsets[:]))

        q_grouped = keep.tile([P, NQ, PACK], BF16, name="q_grouped", align_bytes=64)
        q_codes = keep.tile([P, NQ], U32, name="q_codes", align_bytes=64)
        q_scales = keep.tile([P, NQ], U8, name="q_scales", align_bytes=64)
        nc.scalar.copy(q_grouped[:], q_raw[:].rearrange("p t q -> p q t"))

        kb_turn = psum.tile([P, COLS, P], F32, name="kb_turn", tag="turn")
        for c in range(COLS):
            nc.tensor.transpose(kb_turn[:, c, :], kb_row[:, c * P : (c + 1) * P], ident[:])
        kb_col = keep.tile([P, COLS], F32, name="kb_col")
        nc.scalar.copy(kb_col[:], kb_turn[:, :, 0])
        kb_spread = psum.tile([P, COLS, P], F32, name="kb_spread", tag="turn")
        for c in range(COLS):
            nc.tensor.transpose(kb_spread[:, c, :], kb_col[:, c : c + 1].to_broadcast([P, P]), ident[:])

        nc.vector.quantize_mx(out=q_codes[:].bitcast(FP8X4), scales=q_scales[:], in_=q_grouped[:].rearrange("p q t -> p (q t)"))

        nc.vector.tensor_copy(k_first[:, 1, :], k_win[1][:].indirect(offsets[:]))
        nc.scalar.copy(k_grouped[:, :, 0:2], k_first[:].rearrange("p t i -> p i t"))
        kb_all = keep.tile([P, SLOTS], F32, name="kb_all")
        nc.scalar.copy(kb_all[:], kb_spread[:].rearrange("p c i -> p (c i)"))

        vs_perm = keep.tile([P, PACK, P], F32, name="vs_perm")
        nc.scalar.copy(vs_perm[:].rearrange("p t m -> p m t"), vs_row[:].rearrange("p (m t) -> p m t", t=PACK))
        vs_turn = psum.tile([P, PACK, P], F32, name="vs_turn", tag="turn")
        for t in range(PACK):
            nc.tensor.transpose(vs_turn[:, t, :], vs_perm[:, t, :], ident[:])
        vs_col = keep.tile([P, PACK], F32, name="vs_col")
        nc.scalar.copy(vs_col[:], vs_turn[:, :, 0])

        for t in range(2, PACK):
            nc.vector.tensor_copy(k_grouped[:, :, t], k_win[t][:].indirect(offsets[:]))
        k_codes = keep.tile([P, SLOTS], U32, name="k_codes", align_bytes=64)
        k_scales = keep.tile([P, SLOTS], U8, name="k_scales", align_bytes=64)
        nc.vector.quantize_mx(out=k_codes[:].bitcast(FP8X4), scales=k_scales[:], in_=k_grouped[:].rearrange("p i t -> p (i t)"))
        score = psum.tile([NQ, SLOTS], F32, name="score", tag="score", bufs=1)
        nc.tensor.matmul_mx(
            out=score[:],
            lhsT=q_codes[:].bitcast(FP8X4),
            lhsT_scale=q_scales[:],
            rhs=k_codes[:].bitcast(FP8X4),
            rhs_scale=k_scales[:],
            start=True,
            stop=True,
        )

        gather_values(0)
        turn_values(0)

        neg = keep.tile([NQ, SLOTS], F32, name="neg", tag="v_win0", align_bytes=64)
        nc.vector.scalar_tensor_tensor(neg[:], score[:], -1.0, kb_all[:], mult, subtract)
        neg_m = keep.tile([NQ, 1], F32, name="neg_m")
        nc.vector.tensor_reduce(neg_m[:], neg[:], axis=mybir.AxisListType.X, op=minimum)
        gather_values(1)
        codes_0 = keep.tile([P, P], U32, name="codes_0", align_bytes=64)
        quantize_values(0, 1, codes_0[:])

        p = keep.tile([NQ, PACK, P], F32, name="p")
        total = keep.tile([NQ, 1], F32, name="total")
        nc.scalar.activation(
            p[:].rearrange("q t m -> q m t"),
            neg[:].rearrange("q (m t) -> q m t", t=PACK),
            exp,
            bias=neg_m[:],
            scale=-1.0,
            accum_out=total[:],
        )
        p_turn = psum.tile([P, PACK, NQ], F32, name="p_turn", tag="turn")
        for t in range(PACK):
            nc.tensor.transpose(p_turn[:, t, :], p[:, t, :], ident[:])
        turn_values(1)
        gather_values(2)
        gather_values(3)

        w_grouped = over.tile([P, NQ, PACK], BF16, name="w_grouped", offset=0, align_bytes=64)
        nc.vector.tensor_tensor(
            w_grouped[:],
            p_turn[:].rearrange("m t q -> m q t"),
            vs_col[:].unsqueeze(1).to_broadcast([P, NQ, PACK]),
            mult,
        )
        turn_values(2)
        codes_12 = over.tile([P, 2 * P], U32, name="codes_12", offset=2 * NQ * PACK, align_bytes=64)
        quantize_values(1, 2, codes_12[:])
        w_codes = keep.tile([P, NQ], U32, name="w_codes", align_bytes=64)
        w_scales = keep.tile([P, NQ], U8, name="w_scales", align_bytes=64)
        nc.vector.quantize_mx(out=w_codes[:].bitcast(FP8X4), scales=w_scales[:], in_=w_grouped[:].rearrange("p q t -> p (q t)"))
        inverse = keep.tile([NQ, 1], F32, name="inverse")
        nc.vector.reciprocal(inverse[:], total[:])
        turn_values(3)
        codes_3 = keep.tile([P, P], U32, name="codes_3", align_bytes=64)
        quantize_values(3, 1, codes_3[:])

        def product(y, b):
            nc.tensor.matmul_mx(
                out=y,
                lhsT=w_codes[:].bitcast(FP8X4),
                lhsT_scale=w_scales[:],
                rhs=v_codes[b].bitcast(FP8X4),
                rhs_scale=v_scales[:, b, :],
                start=True,
                stop=True,
            )

        y_first = psum.tile([NQ, 2, P], F32, name="y_first", tag="y")
        y_last = psum.tile([NQ, 2, P], F32, name="y_last", tag="y")
        for b in range(2):
            product(y_first[:, b, :], b)
        out_first = keep.tile([NQ, 2 * P], F32, name="out_first")
        nc.scalar.activation(out_first[:], y_first[:].rearrange("q b e -> q (b e)"), copy, scale=inverse[:])
        nc.scalar.dma_start(out[0, :, 0 : 2 * P], out_first[:])

        for b in range(2):
            product(y_last[:, b, :], 2 + b)
        out_last = keep.tile([NQ, 2 * P], F32, name="out_last")
        nc.vector.tensor_scalar(out_last[:], y_last[:].rearrange("q b e -> q (b e)"), inverse[:], None, mult)
        nc.sync.dma_start(out[0, :, 2 * P : DV], out_last[:])
